import numpy as np
import ml_dtypes

BF16 = ml_dtypes.bfloat16


def bf(x):
    return np.asarray(x, np.float32).astype(BF16)


def f32(x):
    return np.asarray(x, np.float32)


def f64(x):
    return np.asarray(x).astype(np.float64)


def striped(idx):
    return np.tile(idx.reshape(-1, 16).T, (8, 1))


S, K, M, N, B, Q = 512, 128, 128, 512, 4, 128


def setup_inputs():
    return {"base": bf(np.random.standard_normal((B, M, S))), "x": bf(np.random.standard_normal((K, N))), "w": bf(np.random.standard_normal((K, M)) / np.sqrt(K)), "c": f32(0.2 + 0.8 * np.random.random_sample((1, S))), "offs": striped(np.random.permutation(S))}


def reference(base, x, w, c, offs):
    idx = offs[:16].T.reshape(-1)
    z = f64(base).copy()
    for i in range(B):
        z[i][:, idx[i * Q : (i + 1) * Q]] += f64(w).T @ f64(x)[:, i * Q : (i + 1) * Q]
    return z * f64(c)

@@ -1,0 +1,55 @@
+import concourse.mybir as mybir
+from concourse.masks import make_identity
+
+BF16, F32, U16 = mybir.dt.bfloat16, mybir.dt.float32, mybir.dt.uint16
+MULT = mybir.AluOpType.mult
+
+P = 128
+B, S = 4, 512
+N = 512
+Q = N // B
+Q_COLS = Q // 16
+FLOPS = 2 * P * P * N
+
+
+def tile_scatter_matmul_kernel(tc, base, x, w, c, offs, out):
+    nc = tc.nc
+    with (
+        tc.tile_pool(name="held", bufs=1) as held,
+        tc.psum_pool(name="banks", bufs=1) as banks,
+    ):
+        ident = held.tile([P, P], BF16, name="ident")
+        make_identity(nc, ident[:])
+
+        base_sb = [held.tile([P, S], BF16, name=f"base_sb{i}") for i in range(B)]
+        offsets = held.tile([P, N // 16], U16, name="offsets")
+        x_sb = held.tile([P, N], BF16, name="x_sb")
+        w_sb = held.tile([P, P], BF16, name="w_sb")
+        c_all = held.tile([P, S], F32, name="c_all")
+        nc.sync.dma_start(base_sb[0][:], base[0])
+        nc.scalar.dma_start(base_sb[1][:], base[1])
+        nc.sync.dma_start(base_sb[2][:], base[2])
+        nc.scalar.dma_start(base_sb[3][:], base[3])
+        nc.sync.dma_start(offsets[:], offs)
+        nc.scalar.dma_start(w_sb[:], w)
+        nc.sync.dma_start(x_sb[:], x)
+        nc.scalar.dma_start(c_all[:], c.rearrange("o s -> (o s)").partition_broadcast(P))
+
+        windows = [banks.tile([P, S], F32, name=f"window{i}") for i in range(B)]
+        for i in range(B):
+            nc.tensor.matmul(windows[i][:], ident[:], base_sb[i][:], start=True, stop=False)
+
+        for i in range(B):
+            nc.tensor.matmul(
+                windows[i][:].indirect(offsets[:, i * Q_COLS : (i + 1) * Q_COLS]),
+                w_sb[:],
+                x_sb[:, i * Q : (i + 1) * Q],
+                start=False,
+                stop=True,
+            )
+
+        for i in range(B):
+            scaled = held.tile([P, S], F32, name=f"scaled{i}")
+            nc.vector.tensor_tensor(scaled[:], windows[i][:], c_all[:], MULT)
+            queue = nc.sync if i % 2 == 0 else nc.scalar
+            queue.dma_start(out[i], scaled[:])

@@ -50,6 +50,11 @@ def tile_scatter_matmul_kernel(tc, base, x, w, c, offs, out):
 
         for i in range(B):
             scaled = held.tile([P, S], F32, name=f"scaled{i}")
-            nc.vector.tensor_tensor(scaled[:], windows[i][:], c_all[:], MULT)
+            if i == 0:
+                summed = held.tile([P, S], F32, name="summed")
+                nc.scalar.copy(summed[:], windows[i][:])
+                nc.gpsimd.tensor_tensor(scaled[:], summed[:], c_all[:], MULT)
+            else:
+                nc.vector.tensor_tensor(scaled[:], windows[i][:], c_all[:], MULT)
             queue = nc.sync if i % 2 == 0 else nc.scalar
             queue.dma_start(out[i], scaled[:])

@@ -10,6 +10,7 @@ N = 512
 Q = N // B
 Q_COLS = Q // 16
 FLOPS = 2 * P * P * N
+WARM_MATMULS = 12
 
 
 def tile_scatter_matmul_kernel(tc, base, x, w, c, offs, out):
@@ -18,6 +19,12 @@ def tile_scatter_matmul_kernel(tc, base, x, w, c, offs, out):
         tc.tile_pool(name="held", bufs=1) as held,
         tc.psum_pool(name="banks", bufs=1) as banks,
     ):
+        zeros = held.tile([P, P], BF16, name="zeros")
+        nc.gpsimd.memset(zeros[:], 0.0)
+        unread = banks.tile([P, P], F32, name="unread")
+        for r in range(WARM_MATMULS):
+            nc.tensor.matmul(unread[:], zeros[:], zeros[:], start=True, stop=True)
+
         ident = held.tile([P, P], BF16, name="ident")
         make_identity(nc, ident[:])
 
@@ -50,11 +57,6 @@ def tile_scatter_matmul_kernel(tc, base, x, w, c, offs, out):
 
         for i in range(B):
             scaled = held.tile([P, S], F32, name=f"scaled{i}")
-            if i == 0:
-                summed = held.tile([P, S], F32, name="summed")
-                nc.scalar.copy(summed[:], windows[i][:])
-                nc.gpsimd.tensor_tensor(scaled[:], summed[:], c_all[:], MULT)
-            else:
-                nc.vector.tensor_tensor(scaled[:], windows[i][:], c_all[:], MULT)
+            nc.vector.tensor_tensor(scaled[:], windows[i][:], c_all[:], MULT)
             queue = nc.sync if i % 2 == 0 else nc.scalar
             queue.dma_start(out[i], scaled[:])

@@ -32,7 +32,8 @@ def tile_scatter_matmul_kernel(tc, base, x, w, c, offs, out):
         offsets = held.tile([P, N // 16], U16, name="offsets")
         x_sb = held.tile([P, N], BF16, name="x_sb")
         w_sb = held.tile([P, P], BF16, name="w_sb")
-        c_all = held.tile([P, S], F32, name="c_all")
+        c_row = held.tile([1, S], F32, name="c_row")
+        nc.scalar.dma_start(c_row[:], c)
         nc.sync.dma_start(base_sb[0][:], base[0])
         nc.scalar.dma_start(base_sb[1][:], base[1])
         nc.sync.dma_start(base_sb[2][:], base[2])
@@ -40,7 +41,13 @@ def tile_scatter_matmul_kernel(tc, base, x, w, c, offs, out):
         nc.sync.dma_start(offsets[:], offs)
         nc.scalar.dma_start(w_sb[:], w)
         nc.sync.dma_start(x_sb[:], x)
-        nc.scalar.dma_start(c_all[:], c.rearrange("o s -> (o s)").partition_broadcast(P))
+
+        ones_row = held.tile([1, P], F32, name="ones_row")
+        nc.vector.memset(ones_row[:], 1.0)
+        c_bank = banks.tile([P, S], F32, name="c_bank")
+        nc.tensor.matmul(c_bank[:], ones_row[:], c_row[:], start=True, stop=True)
+        c_all = held.tile([P, S], F32, name="c_all")
+        nc.vector.tensor_copy(c_all[:], c_bank[:])
 
         windows = [banks.tile([P, S], F32, name=f"window{i}") for i in range(B)]
         for i in range(B):

@@ -2,7 +2,7 @@ import concourse.mybir as mybir
 from concourse.masks import make_identity
 
 BF16, F32, U16 = mybir.dt.bfloat16, mybir.dt.float32, mybir.dt.uint16
-MULT = mybir.AluOpType.mult
+MULT, SUBTRACT = mybir.AluOpType.mult, mybir.AluOpType.subtract
 
 P = 128
 B, S = 4, 512
@@ -42,16 +42,22 @@ def tile_scatter_matmul_kernel(tc, base, x, w, c, offs, out):
         nc.scalar.dma_start(w_sb[:], w)
         nc.sync.dma_start(x_sb[:], x)
 
-        ones_row = held.tile([1, P], F32, name="ones_row")
+        ones_row = held.tile([1, P], BF16, name="ones_row")
         nc.vector.memset(ones_row[:], 1.0)
+        c_high = c_row[:].bitcast(BF16)[:, 1::2]
+        c_low = held.tile([1, S], BF16, name="c_low")
+        nc.vector.tensor_tensor(c_low[:], c_row[:], c_high, SUBTRACT)
+
         c_bank = banks.tile([P, S], F32, name="c_bank")
-        nc.tensor.matmul(c_bank[:], ones_row[:], c_row[:], start=True, stop=True)
+        windows = [banks.tile([P, S], F32, name=f"window{i}") for i in range(B)]
+        nc.tensor.matmul(c_bank[:], ones_row[:], c_high, start=True, stop=False)
+        for i in range(B):
+            if i == B // 2:
+                nc.tensor.matmul(c_bank[:], ones_row[:], c_low[:], start=False, stop=True)
+            nc.tensor.matmul(windows[i][:], ident[:], base_sb[i][:], start=True, stop=False)
+
         c_all = held.tile([P, S], F32, name="c_all")
         nc.vector.tensor_copy(c_all[:], c_bank[:])
-
-        windows = [banks.tile([P, S], F32, name=f"window{i}") for i in range(B)]
-        for i in range(B):
-            nc.tensor.matmul(windows[i][:], ident[:], base_sb[i][:], start=True, stop=False)
 
         for i in range(B):
             nc.tensor.matmul(

@@ -10,7 +10,7 @@ N = 512
 Q = N // B
 Q_COLS = Q // 16
 FLOPS = 2 * P * P * N
-WARM_MATMULS = 12
+WARM_MATMULS = 16
 
 
 def tile_scatter_matmul_kernel(tc, base, x, w, c, offs, out):

@@ -10,7 +10,7 @@ N = 512
 Q = N // B
 Q_COLS = Q // 16
 FLOPS = 2 * P * P * N
-WARM_MATMULS = 16
+WARM_MATMULS = 4
 
 
 def tile_scatter_matmul_kernel(tc, base, x, w, c, offs, out):
@@ -19,11 +19,17 @@ def tile_scatter_matmul_kernel(tc, base, x, w, c, offs, out):
         tc.tile_pool(name="held", bufs=1) as held,
         tc.psum_pool(name="banks", bufs=1) as banks,
     ):
-        zeros = held.tile([P, P], BF16, name="zeros")
+        zeros = held.tile([P, 16], BF16, name="zeros")
         nc.gpsimd.memset(zeros[:], 0.0)
-        unread = banks.tile([P, P], F32, name="unread")
+        unread = banks.tile([P, S], F32, name="unread")
         for r in range(WARM_MATMULS):
-            nc.tensor.matmul(unread[:], zeros[:], zeros[:], start=True, stop=True)
+            nc.tensor.matmul(
+                unread[:],
+                zeros[:, 0:1].to_broadcast([P, P]),
+                zeros[:, 0:1].to_broadcast([P, S]),
+                start=True,
+                stop=True,
+            )
 
         ident = held.tile([P, P], BF16, name="ident")
         make_identity(nc, ident[:])

@@ -11,6 +11,7 @@ Q = N // B
 Q_COLS = Q // 16
 FLOPS = 2 * P * P * N
 WARM_MATMULS = 4
+PIECE = 64
 
 
 def tile_scatter_matmul_kernel(tc, base, x, w, c, offs, out):
@@ -41,12 +42,12 @@ def tile_scatter_matmul_kernel(tc, base, x, w, c, offs, out):
         c_row = held.tile([1, S], F32, name="c_row")
         nc.scalar.dma_start(c_row[:], c)
         nc.sync.dma_start(base_sb[0][:], base[0])
-        nc.scalar.dma_start(base_sb[1][:], base[1])
-        nc.sync.dma_start(base_sb[2][:], base[2])
-        nc.scalar.dma_start(base_sb[3][:], base[3])
-        nc.sync.dma_start(offsets[:], offs)
         nc.scalar.dma_start(w_sb[:], w)
+        nc.sync.dma_start(offsets[:], offs)
+        nc.scalar.dma_start(base_sb[1][:], base[1])
         nc.sync.dma_start(x_sb[:], x)
+        nc.scalar.dma_start(base_sb[2][:], base[2])
+        nc.sync.dma_start(base_sb[3][:], base[3])
 
         ones_row = held.tile([1, P], BF16, name="ones_row")
         nc.vector.memset(ones_row[:], 1.0)
@@ -56,16 +57,8 @@ def tile_scatter_matmul_kernel(tc, base, x, w, c, offs, out):
 
         c_bank = banks.tile([P, S], F32, name="c_bank")
         windows = [banks.tile([P, S], F32, name=f"window{i}") for i in range(B)]
-        nc.tensor.matmul(c_bank[:], ones_row[:], c_high, start=True, stop=False)
-        for i in range(B):
-            if i == B // 2:
-                nc.tensor.matmul(c_bank[:], ones_row[:], c_low[:], start=False, stop=True)
-            nc.tensor.matmul(windows[i][:], ident[:], base_sb[i][:], start=True, stop=False)
 
-        c_all = held.tile([P, S], F32, name="c_all")
-        nc.vector.tensor_copy(c_all[:], c_bank[:])
-
-        for i in range(B):
+        def scatter(i):
             nc.tensor.matmul(
                 windows[i][:].indirect(offsets[:, i * Q_COLS : (i + 1) * Q_COLS]),
                 w_sb[:],
@@ -73,6 +66,21 @@ def tile_scatter_matmul_kernel(tc, base, x, w, c, offs, out):
                 start=False,
                 stop=True,
             )
+
+        nc.tensor.matmul(c_bank[:], ones_row[:], c_high, start=True, stop=False)
+        nc.tensor.matmul(windows[0][:], ident[:], base_sb[0][:], start=True, stop=False)
+        nc.tensor.matmul(c_bank[:], ones_row[:], c_low[:], start=False, stop=True)
+        scatter(0)
+
+        c_all = held.tile([P, S], F32, name="c_all")
+        nc.vector.tensor_copy(c_all[:], c_bank[:])
+
+        for i in range(1, B):
+            for p in range(S // PIECE):
+                cols = slice(p * PIECE, (p + 1) * PIECE)
+                nc.tensor.matmul(windows[i][:, cols], ident[:], base_sb[i][:, cols], start=(p == 0), stop=False)
+        for i in range(1, B):
+            scatter(i)
 
         for i in range(B):
             scaled = held.tile([P, S], F32, name=f"scaled{i}")

@@ -2,7 +2,7 @@ import concourse.mybir as mybir
 from concourse.masks import make_identity
 
 BF16, F32, U16 = mybir.dt.bfloat16, mybir.dt.float32, mybir.dt.uint16
-MULT, SUBTRACT = mybir.AluOpType.mult, mybir.AluOpType.subtract
+MULT = mybir.AluOpType.mult
 
 P = 128
 B, S = 4, 512
@@ -12,6 +12,7 @@ Q_COLS = Q // 16
 FLOPS = 2 * P * P * N
 WARM_MATMULS = 4
 PIECE = 64
+C_COLS = S // P
 
 
 def tile_scatter_matmul_kernel(tc, base, x, w, c, offs, out):
@@ -32,15 +33,17 @@ def tile_scatter_matmul_kernel(tc, base, x, w, c, offs, out):
                 stop=True,
             )
 
+        ident_f32 = held.tile([P, P], F32, name="ident_f32")
+        make_identity(nc, ident_f32[:])
         ident = held.tile([P, P], BF16, name="ident")
-        make_identity(nc, ident[:])
+        nc.vector.tensor_copy(ident[:], ident_f32[:])
 
         base_sb = [held.tile([P, S], BF16, name=f"base_sb{i}") for i in range(B)]
         offsets = held.tile([P, N // 16], U16, name="offsets")
         x_sb = held.tile([P, N], BF16, name="x_sb")
         w_sb = held.tile([P, P], BF16, name="w_sb")
-        c_row = held.tile([1, S], F32, name="c_row")
-        nc.scalar.dma_start(c_row[:], c)
+        c_cols = held.tile([P, C_COLS], F32, name="c_cols")
+        nc.scalar.dma_start(c_cols[:], c.rearrange("o (p a) -> p (o a)", a=C_COLS))
         nc.sync.dma_start(base_sb[0][:], base[0])
         nc.scalar.dma_start(w_sb[:], w)
         nc.sync.dma_start(offsets[:], offs)
@@ -48,12 +51,6 @@ def tile_scatter_matmul_kernel(tc, base, x, w, c, offs, out):
         nc.sync.dma_start(x_sb[:], x)
         nc.scalar.dma_start(base_sb[2][:], base[2])
         nc.sync.dma_start(base_sb[3][:], base[3])
-
-        ones_row = held.tile([1, P], BF16, name="ones_row")
-        nc.vector.memset(ones_row[:], 1.0)
-        c_high = c_row[:].bitcast(BF16)[:, 1::2]
-        c_low = held.tile([1, S], BF16, name="c_low")
-        nc.vector.tensor_tensor(c_low[:], c_row[:], c_high, SUBTRACT)
 
         c_bank = banks.tile([P, S], F32, name="c_bank")
         windows = [banks.tile([P, S], F32, name=f"window{i}") for i in range(B)]
@@ -67,13 +64,20 @@ def tile_scatter_matmul_kernel(tc, base, x, w, c, offs, out):
                 stop=True,
             )
 
-        nc.tensor.matmul(c_bank[:], ones_row[:], c_high, start=True, stop=False)
+        for a in range(C_COLS):
+            nc.tensor.transpose(
+                c_bank[:, a * P : (a + 1) * P],
+                c_cols[:, a : a + 1].to_broadcast([P, P]),
+                ident_f32[:],
+            )
         nc.tensor.matmul(windows[0][:], ident[:], base_sb[0][:], start=True, stop=False)
-        nc.tensor.matmul(c_bank[:], ones_row[:], c_low[:], start=False, stop=True)
         scatter(0)
 
         c_all = held.tile([P, S], F32, name="c_all")
-        nc.vector.tensor_copy(c_all[:], c_bank[:])
+        nc.vector.tensor_copy(
+            c_all[:].rearrange("m (p a) -> m p a", a=C_COLS),
+            c_bank[:].rearrange("m (a p) -> m p a", a=C_COLS),
+        )
 
         for i in range(1, B):
             for p in range(S // PIECE):

@@ -11,7 +11,7 @@ Q = N // B
 Q_COLS = Q // 16
 FLOPS = 2 * P * P * N
 WARM_MATMULS = 4
-PIECE = 64
+PIECE = 40
 C_COLS = S // P
 
 
@@ -70,8 +70,10 @@ def tile_scatter_matmul_kernel(tc, base, x, w, c, offs, out):
                 c_cols[:, a : a + 1].to_broadcast([P, P]),
                 ident_f32[:],
             )
-        nc.tensor.matmul(windows[0][:], ident[:], base_sb[0][:], start=True, stop=False)
-        scatter(0)
+        for i in (0, 1):
+            nc.tensor.matmul(windows[i][:], ident[:], base_sb[i][:], start=True, stop=False)
+        for i in (0, 1):
+            scatter(i)
 
         c_all = held.tile([P, S], F32, name="c_all")
         nc.vector.tensor_copy(
@@ -79,11 +81,11 @@ def tile_scatter_matmul_kernel(tc, base, x, w, c, offs, out):
             c_bank[:].rearrange("m (a p) -> m p a", a=C_COLS),
         )
 
-        for i in range(1, B):
-            for p in range(S // PIECE):
-                cols = slice(p * PIECE, (p + 1) * PIECE)
-                nc.tensor.matmul(windows[i][:, cols], ident[:], base_sb[i][:, cols], start=(p == 0), stop=False)
-        for i in range(1, B):
+        for i in (2, 3):
+            for left in range(0, S, PIECE):
+                cols = slice(left, min(left + PIECE, S))
+                nc.tensor.matmul(windows[i][:, cols], ident[:], base_sb[i][:, cols], start=(left == 0), stop=False)
+        for i in (2, 3):
             scatter(i)
 
         for i in range(B):

import concourse.mybir as mybir
from concourse.masks import make_identity

BF16, F32, U16 = mybir.dt.bfloat16, mybir.dt.float32, mybir.dt.uint16
MULT = mybir.AluOpType.mult

P = 128
B, S = 4, 512
N = 512
Q = N // B
Q_COLS = Q // 16
FLOPS = 2 * P * P * N
WARM_MATMULS = 4
PIECE = 40
C_COLS = S // P


def tile_scatter_matmul_kernel(tc, base, x, w, c, offs, out):
    nc = tc.nc
    with (
        tc.tile_pool(name="held", bufs=1) as held,
        tc.psum_pool(name="banks", bufs=1) as banks,
    ):
        zeros = held.tile([P, 16], BF16, name="zeros")
        nc.gpsimd.memset(zeros[:], 0.0)
        unread = banks.tile([P, S], F32, name="unread")
        for r in range(WARM_MATMULS):
            nc.tensor.matmul(
                unread[:],
                zeros[:, 0:1].to_broadcast([P, P]),
                zeros[:, 0:1].to_broadcast([P, S]),
                start=True,
                stop=True,
            )

        ident_f32 = held.tile([P, P], F32, name="ident_f32")
        make_identity(nc, ident_f32[:])
        ident = held.tile([P, P], BF16, name="ident")
        nc.vector.tensor_copy(ident[:], ident_f32[:])

        base_sb = [held.tile([P, S], BF16, name=f"base_sb{i}") for i in range(B)]
        offsets = held.tile([P, N // 16], U16, name="offsets")
        x_sb = held.tile([P, N], BF16, name="x_sb")
        w_sb = held.tile([P, P], BF16, name="w_sb")
        c_cols = held.tile([P, C_COLS], F32, name="c_cols")
        nc.scalar.dma_start(c_cols[:], c.rearrange("o (p a) -> p (o a)", a=C_COLS))
        nc.sync.dma_start(base_sb[0][:], base[0])
        nc.scalar.dma_start(w_sb[:], w)
        nc.sync.dma_start(offsets[:], offs)
        nc.scalar.dma_start(base_sb[1][:], base[1])
        nc.sync.dma_start(x_sb[:], x)
        nc.scalar.dma_start(base_sb[2][:], base[2])
        nc.sync.dma_start(base_sb[3][:], base[3])

        c_bank = banks.tile([P, S], F32, name="c_bank")
        windows = [banks.tile([P, S], F32, name=f"window{i}") for i in range(B)]

        def scatter(i):
            nc.tensor.matmul(
                windows[i][:].indirect(offsets[:, i * Q_COLS : (i + 1) * Q_COLS]),
                w_sb[:],
                x_sb[:, i * Q : (i + 1) * Q],
                start=False,
                stop=True,
            )

        for a in range(C_COLS):
            nc.tensor.transpose(
                c_bank[:, a * P : (a + 1) * P],
                c_cols[:, a : a + 1].to_broadcast([P, P]),
                ident_f32[:],
            )
        for i in (0, 1):
            nc.tensor.matmul(windows[i][:], ident[:], base_sb[i][:], start=True, stop=False)
        for i in (0, 1):
            scatter(i)

        c_all = held.tile([P, S], F32, name="c_all")
        nc.vector.tensor_copy(
            c_all[:].rearrange("m (p a) -> m p a", a=C_COLS),
            c_bank[:].rearrange("m (a p) -> m p a", a=C_COLS),
        )

        for i in (2, 3):
            for left in range(0, S, PIECE):
                cols = slice(left, min(left + PIECE, S))
                nc.tensor.matmul(windows[i][:, cols], ident[:], base_sb[i][:, cols], start=(left == 0), stop=False)
        for i in (2, 3):
            scatter(i)

        for i in range(B):
            scaled = held.tile([P, S], F32, name=f"scaled{i}")
            nc.vector.tensor_tensor(scaled[:], windows[i][:], c_all[:], MULT)
            queue = nc.sync if i % 2 == 0 else nc.scalar
            queue.dma_start(out[i], scaled[:])
